import numpy as np, ml_dtypes
CORES = [122,123,126,250,251,254,378,379,382,506,507,510]
N = 12
F = 128
GROUPS = [[0,6,9],[3,4,7],[2,10,11],[1,5,8]]
def setup_inputs(rng):
    return {"x": rng.standard_normal((N, 128, F), dtype=np.float32).astype(ml_dtypes.bfloat16), "w": (rng.standard_normal((N, 128, 128), dtype=np.float32) / 11).astype(ml_dtypes.bfloat16)}
def setup_inputs_big(rng):
    d = setup_inputs(rng)
    for k in ("x", "w"): d[k] = (d[k].astype(np.float32) * 1024.0).astype(d[k].dtype)
    return d
def setup_inputs_small(rng):
    d = setup_inputs(rng)
    for k in ("x", "w"): d[k] = (d[k].astype(np.float32) * (1 / 1024.0)).astype(d[k].dtype)
    return d
def setup_inputs_apart(rng):
    d = setup_inputs(rng)
    f = (10.0 ** rng.permutation(np.linspace(-1.5, 1.5, N))).astype(np.float32).reshape(N, 1, 1)
    for k in ("x", "w"): d[k] = (d[k].astype(np.float32) * f).astype(d[k].dtype)
    return d
def reference(x, w):
    X, W = x.astype(np.float64), w.astype(np.float64)
    s = sum(W[g[0]].T @ np.maximum(sum(X[j] for j in g), 0.0) for g in GROUPS).astype(ml_dtypes.bfloat16)
    return {"y": np.broadcast_to(s, (N,) + s.shape)}

@@ -1,0 +1,185 @@
+from concourse.bass import DstId, RemoteDMATransfer
+from concourse.mybir import AluOpType
+
+F = 128
+NENG = 8
+
+SCRATCH = {
+    "xw": ("sbuf", [128, 2 * F], "bfloat16"),
+    "inW": ("sbuf", [128, 2 * F], "bfloat16"),
+    "inA": ("sbuf", [128, F], "bfloat16"),
+    "inB": ("sbuf", [128, F], "bfloat16"),
+    "zero": ("sbuf", [128, F], "float32"),
+    "tsb": ("sbuf", [128, F], "bfloat16"),
+    "psb": ("sbuf", [128, F], "bfloat16"),
+    "ps1": ("psum", [128, 512], "float32"),
+    "ps2": ("psum", [128, 512], "float32"),
+    "ps3": ("psum", [128, 512], "float32"),
+    "pland": ("dram", [4, 128, F], "bfloat16"),
+    "pown": ("sbuf", [128, 4 * F], "bfloat16"),
+    "ysb": ("sbuf", [128, F], "bfloat16"),
+    "yland": ("dram", [128, F], "bfloat16"),
+}
+SEMAPHORES = ["ld", "sent", "sW", "sA", "sB", "zs", "va", "vb", "vt", "mm", "cp",
+              "parr0", "parr1", "parr2", "parr3", "pl0", "pl1", "pl2", "pl3", "yarr", "st"]
+
+
+def _perms(items, k):
+    if k == 0:
+        return [[]]
+    out = []
+    for i, a in enumerate(items):
+        for rest in _perms(items[:i] + items[i + 1:], k - 1):
+            out.append([a] + rest)
+    return out
+
+
+def _plan(T, topo):
+    cores = list(T.cores)
+    groups = T.tables["GROUPS"]
+    host_of = [topo.host(c) for c in cores]
+    hosts = sorted(set(host_of))
+    at = {h: [r for r in range(len(cores)) if host_of[r] == h] for h in hosts}
+
+    def near(a, b):
+        return a == b or all(topo.may_write(cores[i], cores[j]) for i in at[a] for j in at[b])
+
+    meet = [[h for h in hosts if all(near(host_of[j], h) for j in grp)] for grp in groups]
+    pair, chost = None, None
+    for i, a in enumerate(hosts):
+        for b in hosts[i + 1:]:
+            if pair is not None or not all(near(a, h) or near(b, h) for h in hosts):
+                continue
+            ch = [[h for h in m if near(h, a) and near(h, b)] for m in meet]
+            if all(ch):
+                pair, chost = (a, b), [c[0] for c in ch]
+    firsts = [grp[0] for grp in groups]
+    centre = [None] * len(groups)
+    for h in hosts:
+        gs = [k for k in range(len(groups)) if chost[k] == h]
+        best, bs = None, None
+        for pick in _perms(at[h], len(gs)):
+            s = (100 * sum(1 for i, r in enumerate(pick) if r not in groups[gs[i]])
+                 + 10 * len(set(topo.die(cores[r]) for r in pick))
+                 - sum(1 for r in pick if r in firsts))
+            if best is None or s > bs:
+                best, bs = pick, s
+        for i, k in enumerate(gs):
+            centre[k] = best[i]
+    asm = []
+    for a in pair:
+        asm.append(min(at[a], key=lambda r: sum(1 for q in at[a] if topo.die(cores[q]) != topo.die(cores[r]))))
+    serve = {m: [r for r in at[host_of[m]] if r != m] for m in asm}
+    for h in hosts:
+        if h in pair:
+            continue
+        cand = [m for m in asm if near(host_of[m], h)]
+        cand.sort(key=lambda m: 0 if topo.same_plane(cores[m], cores[at[h][0]]) else 1)
+        rs = sorted(at[h], key=lambda r: 0 if topo.die(cores[r]) == topo.die(cores[cand[0]]) else 1)
+        k = len(rs) if len(cand) == 1 else (2 * len(rs) + 2) // 3
+        serve[cand[0]] += rs[:k]
+        if len(cand) > 1:
+            serve[cand[1]] += rs[k:]
+    return centre, asm, serve
+
+
+def _engines(allowed, n):
+    out, k, b = 0, 0, 0
+    while k < n:
+        if (allowed >> b) & 1:
+            out |= 1 << b
+            k += 1
+        b += 1
+    return out
+
+
+def rank_program(g, core, T, topo):
+    rank = T.rank_of(core)
+    if rank is None:
+        return
+    S = T.sem
+    cores = list(T.cores)
+    groups = T.tables["GROUPS"]
+    centre, asm, serve = _plan(T, topo)
+    mine = [k for k in range(len(groups)) if rank in groups[k]][0]
+    work = [k for k in range(len(groups)) if centre[k] == rank]
+    first = groups[mine][0] == rank
+
+    dests = [centre[mine]] + (list(asm) if work else []) + (serve[rank] if rank in asm else [])
+    allowed = topo.mask(core, cores[dests[0]])
+    for d in dests:
+        allowed &= topo.mask(core, cores[d])
+    n = min(NENG, bin(allowed).count("1"))
+    eng = _engines(allowed, n)
+
+    def dst(r):
+        rid, pid = topo.addr(cores[r], core)
+        return DstId(rid=rid, pnc=pid)
+
+    g.sync.dma_start(out=T.xw[:, 0:F], in_=T.x[:, :]).then_inc(S.ld, 16)
+    if first:
+        g.scalar.dma_start(out=T.xw[:, F:2 * F], in_=T.w[:, :]).then_inc(S.ld, 16)
+    g.wait_ge(S.ld, 32 if first else 16)
+    rid, pid = topo.addr(cores[centre[mine]], core)
+    slot = groups[mine].index(rank)
+    if first:
+        g.remote_dma(out_ap=T.inW[:, :], in_ap=T.xw[:, :], remote_sem=S.sW, local_sem=S.sent,
+                     pid=pid, routing_id=rid, dma_engine_mask=eng)
+    else:
+        g.remote_dma(out_ap=(T.inA if slot == 1 else T.inB)[:, :], in_ap=T.xw[:, 0:F],
+                     remote_sem=(S.sA if slot == 1 else S.sB), local_sem=S.sent,
+                     pid=pid, routing_id=rid, dma_engine_mask=eng)
+    sent = n
+
+    v = g.vector
+    if work:
+        k = work[0]
+        v.memset(T.zero[:, :], 0.0).then_inc(S.zs, 1)
+        v.wait_ge(S.sA, n)
+        v.wait_ge(S.sB, n)
+        v.tensor_tensor(out=T.ps1[:, 0:F], in0=T.inA[:, :], in1=T.inB[:, :], op=AluOpType.add).then_inc(S.va, 1)
+        v.wait_ge(S.sW, n)
+        v.wait_ge(S.va, 1)
+        v.tensor_tensor(out=T.ps2[:, 0:F], in0=T.ps1[:, 0:F], in1=T.inW[:, 0:F], op=AluOpType.add).then_inc(S.vb, 1)
+        v.wait_ge(S.zs, 1)
+        v.wait_ge(S.vb, 1)
+        v.tensor_tensor(out=T.tsb[:, :], in0=T.ps2[:, 0:F], in1=T.zero[:, :], op=AluOpType.max).then_inc(S.vt, 1)
+        g.tensor.wait_ge(S.sW, n)
+        g.tensor.wait_ge(S.vt, 1)
+        g.tensor.matmul(out=T.ps3[:, 0:F], lhsT=T.inW[:, F:2 * F], rhs=T.tsb[:, :], start=True, stop=True).then_inc(S.mm, 1)
+        v.wait_ge(S.mm, 1)
+        v.tensor_copy(out=T.psb[:, :], in_=T.ps3[:, 0:F]).then_inc(S.cp, 1)
+        g.wait_ge(S.cp, 1)
+        g.remote_dma_fused([RemoteDMATransfer(dst_ids=[dst(m) for m in asm], dma_engine_mask=eng,
+                                              remote_sem=S["parr%d" % k], srcs=[T.psb[:, :]],
+                                              dsts=[T.pland[k] for m in asm], alu_op=0)], local_sem=S.sent)
+        sent += n
+
+    if rank in asm:
+        G = len(groups)
+        for k in range(G):
+            q = g.sync if k % 2 == 0 else g.scalar
+            q.wait_ge(S["parr%d" % k], n)
+            q.dma_start(out=T.pown[:, k * F:(k + 1) * F], in_=T.pland[k]).then_inc(S["pl%d" % k], 16)
+        for k in range(G):
+            g.wait_ge(S["parr%d" % k], n)
+        g.remote_dma_fused([RemoteDMATransfer(dst_ids=[dst(r) for r in serve[rank]], dma_engine_mask=eng,
+                                              remote_sem=S.yarr, srcs=[T.pland[k] for k in range(G)],
+                                              dsts=[T.yland[:, :] for r in serve[rank]], alu_op=1)], local_sem=S.sent)
+        sent += n
+        v.wait_ge(S.pl0, 16)
+        v.wait_ge(S.pl1, 16)
+        v.tensor_tensor(out=T.ps1[:, 0:F], in0=T.pown[:, 0:F], in1=T.pown[:, F:2 * F], op=AluOpType.add).then_inc(S.va, 1)
+        v.wait_ge(S.pl2, 16)
+        v.wait_ge(S.va, 1)
+        v.tensor_tensor(out=T.ps2[:, 0:F], in0=T.ps1[:, 0:F], in1=T.pown[:, 2 * F:3 * F], op=AluOpType.add).then_inc(S.vb, 1)
+        v.wait_ge(S.pl3, 16)
+        v.wait_ge(S.vb, 1)
+        v.tensor_tensor(out=T.ysb[:, :], in0=T.ps2[:, 0:F], in1=T.pown[:, 3 * F:4 * F], op=AluOpType.add).then_inc(S.vt, 1)
+        g.sync.wait_ge(S.vt, 1)
+        g.sync.dma_start(out=T.y[:, :], in_=T.ysb[:, :]).then_inc(S.st, 16)
+    else:
+        g.sync.wait_ge(S.yarr, n)
+        g.sync.dma_start(out=T.y[:, :], in_=T.yland[:, :]).then_inc(S.st, 16)
+    g.sync.wait_ge(S.st, 16)
+    g.wait_ge(S.sent, sent)

@@ -21,7 +21,7 @@ SCRATCH = {
     "yland": ("dram", [128, F], "bfloat16"),
 }
 SEMAPHORES = ["ld", "sent", "sW", "sA", "sB", "zs", "va", "vb", "vt", "mm", "cp",
-              "parr0", "parr1", "parr2", "parr3", "pl0", "pl1", "pl2", "pl3", "yarr", "st"]
+              "parr0", "parr1", "parr2", "parr3", "qarr0", "qarr1", "qarr2", "qarr3", "yarr", "st"]
 
 
 def _perms(items, k):
@@ -111,10 +111,15 @@ def rank_program(g, core, T, topo):
         allowed &= topo.mask(core, cores[d])
     n = min(NENG, bin(allowed).count("1"))
     eng = _engines(allowed, n)
+    h = n // 2
+    halves = (_engines(eng, h), eng & ~_engines(eng, h))
 
     def dst(r):
         rid, pid = topo.addr(cores[r], core)
         return DstId(rid=rid, pnc=pid)
+
+    def one_chip(a, b):
+        return topo.host(a) == topo.host(b) and topo.chip(a) == topo.chip(b)
 
     g.sync.dma_start(out=T.xw[:, 0:F], in_=T.x[:, :]).then_inc(S.ld, 16)
     if first:
@@ -150,36 +155,44 @@ def rank_program(g, core, T, topo):
         v.wait_ge(S.mm, 1)
         v.tensor_copy(out=T.psb[:, :], in_=T.ps3[:, 0:F]).then_inc(S.cp, 1)
         g.wait_ge(S.cp, 1)
-        g.remote_dma_fused([RemoteDMATransfer(dst_ids=[dst(m) for m in asm], dma_engine_mask=eng,
-                                              remote_sem=S["parr%d" % k], srcs=[T.psb[:, :]],
-                                              dsts=[T.pland[k] for m in asm], alu_op=0)], local_sem=S.sent)
-        sent += n
+        for sem, land in ((S["parr%d" % k], T.pland[k]), (S["qarr%d" % k], T.pown[:, k * F:(k + 1) * F])):
+            g.remote_dma_fused([RemoteDMATransfer(dst_ids=[dst(m)], dma_engine_mask=halves[i], remote_sem=sem,
+                                                  srcs=[T.psb[:, :]], dsts=[land], alu_op=0)
+                                for i, m in enumerate(asm)], local_sem=S.sent)
+            sent += 2 * h
 
     if rank in asm:
         G = len(groups)
         for k in range(G):
-            q = g.sync if k % 2 == 0 else g.scalar
-            q.wait_ge(S["parr%d" % k], n)
-            q.dma_start(out=T.pown[:, k * F:(k + 1) * F], in_=T.pland[k]).then_inc(S["pl%d" % k], 16)
-        for k in range(G):
-            g.wait_ge(S["parr%d" % k], n)
-        g.remote_dma_fused([RemoteDMATransfer(dst_ids=[dst(r) for r in serve[rank]], dma_engine_mask=eng,
-                                              remote_sem=S.yarr, srcs=[T.pland[k] for k in range(G)],
-                                              dsts=[T.yland[:, :] for r in serve[rank]], alu_op=1)], local_sem=S.sent)
-        sent += n
-        v.wait_ge(S.pl0, 16)
-        v.wait_ge(S.pl1, 16)
+            g.wait_ge(S["parr%d" % k], h)
+        near_rs = [r for r in serve[rank] if one_chip(core, cores[r])]
+        plane = [r for r in serve[rank] if topo.same_plane(core, cores[r])]
+        cable = [r for r in serve[rank] if r not in near_rs and r not in plane]
+        spare = ~eng
+        for r in near_rs:
+            spare &= topo.mask(core, cores[r])
+
+        def fold(rs, e):
+            return RemoteDMATransfer(dst_ids=[dst(r) for r in rs], dma_engine_mask=e, remote_sem=S.yarr,
+                                     srcs=[T.pland[k] for k in range(G)], dsts=[T.yland[:, :] for r in rs], alu_op=1)
+
+        g.remote_dma_fused([fold(plane, halves[0]), fold(cable, halves[1])], local_sem=S.sent)
+        g.remote_dma_fused([fold(near_rs, _engines(spare, n))], local_sem=S.sent)
+        sent += 2 * h + n
+        v.wait_ge(S.qarr0, h)
+        v.wait_ge(S.qarr1, h)
         v.tensor_tensor(out=T.ps1[:, 0:F], in0=T.pown[:, 0:F], in1=T.pown[:, F:2 * F], op=AluOpType.add).then_inc(S.va, 1)
-        v.wait_ge(S.pl2, 16)
+        v.wait_ge(S.qarr2, h)
         v.wait_ge(S.va, 1)
         v.tensor_tensor(out=T.ps2[:, 0:F], in0=T.ps1[:, 0:F], in1=T.pown[:, 2 * F:3 * F], op=AluOpType.add).then_inc(S.vb, 1)
-        v.wait_ge(S.pl3, 16)
+        v.wait_ge(S.qarr3, h)
         v.wait_ge(S.vb, 1)
         v.tensor_tensor(out=T.ysb[:, :], in0=T.ps2[:, 0:F], in1=T.pown[:, 3 * F:4 * F], op=AluOpType.add).then_inc(S.vt, 1)
         g.sync.wait_ge(S.vt, 1)
         g.sync.dma_start(out=T.y[:, :], in_=T.ysb[:, :]).then_inc(S.st, 16)
     else:
-        g.sync.wait_ge(S.yarr, n)
+        giver = [m for m in asm if rank in serve[m]][0]
+        g.sync.wait_ge(S.yarr, n if one_chip(core, cores[giver]) else h)
         g.sync.dma_start(out=T.y[:, :], in_=T.yland[:, :]).then_inc(S.st, 16)
     g.sync.wait_ge(S.st, 16)
     g.wait_ge(S.sent, sent)

@@ -5,8 +5,10 @@ F = 128
 NENG = 8
 
 SCRATCH = {
-    "xw": ("sbuf", [128, 2 * F], "bfloat16"),
-    "inW": ("sbuf", [128, 2 * F], "bfloat16"),
+    "xd": ("dram", [128, F], "bfloat16"),
+    "wd": ("dram", [128, F], "bfloat16"),
+    "inX": ("sbuf", [128, F], "bfloat16"),
+    "inW": ("sbuf", [128, F], "bfloat16"),
     "inA": ("sbuf", [128, F], "bfloat16"),
     "inB": ("sbuf", [128, F], "bfloat16"),
     "zero": ("sbuf", [128, F], "float32"),
@@ -20,7 +22,7 @@ SCRATCH = {
     "ysb": ("sbuf", [128, F], "bfloat16"),
     "yland": ("dram", [128, F], "bfloat16"),
 }
-SEMAPHORES = ["ld", "sent", "sW", "sA", "sB", "zs", "va", "vb", "vt", "mm", "cp",
+SEMAPHORES = ["ld", "ldw", "sent", "sX", "sW", "sA", "sB", "zs", "va", "vb", "vt", "mm", "cp",
               "parr0", "parr1", "parr2", "parr3", "qarr0", "qarr1", "qarr2", "qarr3", "yarr", "st"]
 
 
@@ -121,20 +123,21 @@ def rank_program(g, core, T, topo):
     def one_chip(a, b):
         return topo.host(a) == topo.host(b) and topo.chip(a) == topo.chip(b)
 
-    g.sync.dma_start(out=T.xw[:, 0:F], in_=T.x[:, :]).then_inc(S.ld, 16)
+    g.sync.dma_start(out=T.xd[:, :], in_=T.x[:, :]).then_inc(S.ld, 16)
     if first:
-        g.scalar.dma_start(out=T.xw[:, F:2 * F], in_=T.w[:, :]).then_inc(S.ld, 16)
-    g.wait_ge(S.ld, 32 if first else 16)
+        g.scalar.dma_start(out=T.wd[:, :], in_=T.w[:, :]).then_inc(S.ldw, 16)
     rid, pid = topo.addr(cores[centre[mine]], core)
     slot = groups[mine].index(rank)
-    if first:
-        g.remote_dma(out_ap=T.inW[:, :], in_ap=T.xw[:, :], remote_sem=S.sW, local_sem=S.sent,
-                     pid=pid, routing_id=rid, dma_engine_mask=eng)
-    else:
-        g.remote_dma(out_ap=(T.inA if slot == 1 else T.inB)[:, :], in_ap=T.xw[:, 0:F],
-                     remote_sem=(S.sA if slot == 1 else S.sB), local_sem=S.sent,
-                     pid=pid, routing_id=rid, dma_engine_mask=eng)
+    g.wait_ge(S.ld, 16)
+    g.remote_dma(out_ap=(T.inX, T.inA, T.inB)[slot][:, :], in_ap=T.xd[:, :],
+                 remote_sem=(S.sX, S.sA, S.sB)[slot], local_sem=S.sent,
+                 pid=pid, routing_id=rid, dma_engine_mask=eng)
     sent = n
+    if first:
+        g.wait_ge(S.ldw, 16)
+        g.remote_dma(out_ap=T.inW[:, :], in_ap=T.wd[:, :], remote_sem=S.sW, local_sem=S.sent,
+                     pid=pid, routing_id=rid, dma_engine_mask=eng)
+        sent += n
 
     v = g.vector
     if work:
@@ -143,15 +146,15 @@ def rank_program(g, core, T, topo):
         v.wait_ge(S.sA, n)
         v.wait_ge(S.sB, n)
         v.tensor_tensor(out=T.ps1[:, 0:F], in0=T.inA[:, :], in1=T.inB[:, :], op=AluOpType.add).then_inc(S.va, 1)
-        v.wait_ge(S.sW, n)
+        v.wait_ge(S.sX, n)
         v.wait_ge(S.va, 1)
-        v.tensor_tensor(out=T.ps2[:, 0:F], in0=T.ps1[:, 0:F], in1=T.inW[:, 0:F], op=AluOpType.add).then_inc(S.vb, 1)
+        v.tensor_tensor(out=T.ps2[:, 0:F], in0=T.ps1[:, 0:F], in1=T.inX[:, :], op=AluOpType.add).then_inc(S.vb, 1)
         v.wait_ge(S.zs, 1)
         v.wait_ge(S.vb, 1)
         v.tensor_tensor(out=T.tsb[:, :], in0=T.ps2[:, 0:F], in1=T.zero[:, :], op=AluOpType.max).then_inc(S.vt, 1)
         g.tensor.wait_ge(S.sW, n)
         g.tensor.wait_ge(S.vt, 1)
-        g.tensor.matmul(out=T.ps3[:, 0:F], lhsT=T.inW[:, F:2 * F], rhs=T.tsb[:, :], start=True, stop=True).then_inc(S.mm, 1)
+        g.tensor.matmul(out=T.ps3[:, 0:F], lhsT=T.inW[:, :], rhs=T.tsb[:, :], start=True, stop=True).then_inc(S.mm, 1)
         v.wait_ge(S.mm, 1)
         v.tensor_copy(out=T.psb[:, :], in_=T.ps3[:, 0:F]).then_inc(S.cp, 1)
         g.wait_ge(S.cp, 1)

from concourse.bass import DstId, RemoteDMATransfer
from concourse.mybir import AluOpType

F = 128
NENG = 8

SCRATCH = {
    "xd": ("dram", [128, F], "bfloat16"),
    "wd": ("dram", [128, F], "bfloat16"),
    "inX": ("sbuf", [128, F], "bfloat16"),
    "inW": ("sbuf", [128, F], "bfloat16"),
    "inA": ("sbuf", [128, F], "bfloat16"),
    "inB": ("sbuf", [128, F], "bfloat16"),
    "zero": ("sbuf", [128, F], "float32"),
    "tsb": ("sbuf", [128, F], "bfloat16"),
    "psb": ("sbuf", [128, F], "bfloat16"),
    "ps1": ("psum", [128, 512], "float32"),
    "ps2": ("psum", [128, 512], "float32"),
    "ps3": ("psum", [128, 512], "float32"),
    "pland": ("dram", [4, 128, F], "bfloat16"),
    "pown": ("sbuf", [128, 4 * F], "bfloat16"),
    "ysb": ("sbuf", [128, F], "bfloat16"),
    "yland": ("dram", [128, F], "bfloat16"),
}
SEMAPHORES = ["ld", "ldw", "sent", "sX", "sW", "sA", "sB", "zs", "va", "vb", "vt", "mm", "cp",
              "parr0", "parr1", "parr2", "parr3", "qarr0", "qarr1", "qarr2", "qarr3", "yarr", "st"]


def _perms(items, k):
    if k == 0:
        return [[]]
    out = []
    for i, a in enumerate(items):
        for rest in _perms(items[:i] + items[i + 1:], k - 1):
            out.append([a] + rest)
    return out


def _plan(T, topo):
    cores = list(T.cores)
    groups = T.tables["GROUPS"]
    host_of = [topo.host(c) for c in cores]
    hosts = sorted(set(host_of))
    at = {h: [r for r in range(len(cores)) if host_of[r] == h] for h in hosts}

    def near(a, b):
        return a == b or all(topo.may_write(cores[i], cores[j]) for i in at[a] for j in at[b])

    meet = [[h for h in hosts if all(near(host_of[j], h) for j in grp)] for grp in groups]
    pair, chost = None, None
    for i, a in enumerate(hosts):
        for b in hosts[i + 1:]:
            if pair is not None or not all(near(a, h) or near(b, h) for h in hosts):
                continue
            ch = [[h for h in m if near(h, a) and near(h, b)] for m in meet]
            if all(ch):
                pair, chost = (a, b), [c[0] for c in ch]
    firsts = [grp[0] for grp in groups]
    centre = [None] * len(groups)
    for h in hosts:
        gs = [k for k in range(len(groups)) if chost[k] == h]
        best, bs = None, None
        for pick in _perms(at[h], len(gs)):
            s = (100 * sum(1 for i, r in enumerate(pick) if r not in groups[gs[i]])
                 + 10 * len(set(topo.die(cores[r]) for r in pick))
                 - sum(1 for r in pick if r in firsts))
            if best is None or s > bs:
                best, bs = pick, s
        for i, k in enumerate(gs):
            centre[k] = best[i]
    asm = []
    for a in pair:
        asm.append(min(at[a], key=lambda r: sum(1 for q in at[a] if topo.die(cores[q]) != topo.die(cores[r]))))
    serve = {m: [r for r in at[host_of[m]] if r != m] for m in asm}
    for h in hosts:
        if h in pair:
            continue
        cand = [m for m in asm if near(host_of[m], h)]
        cand.sort(key=lambda m: 0 if topo.same_plane(cores[m], cores[at[h][0]]) else 1)
        rs = sorted(at[h], key=lambda r: 0 if topo.die(cores[r]) == topo.die(cores[cand[0]]) else 1)
        k = len(rs) if len(cand) == 1 else (2 * len(rs) + 2) // 3
        serve[cand[0]] += rs[:k]
        if len(cand) > 1:
            serve[cand[1]] += rs[k:]
    return centre, asm, serve


def _engines(allowed, n):
    out, k, b = 0, 0, 0
    while k < n:
        if (allowed >> b) & 1:
            out |= 1 << b
            k += 1
        b += 1
    return out


def rank_program(g, core, T, topo):
    rank = T.rank_of(core)
    if rank is None:
        return
    S = T.sem
    cores = list(T.cores)
    groups = T.tables["GROUPS"]
    centre, asm, serve = _plan(T, topo)
    mine = [k for k in range(len(groups)) if rank in groups[k]][0]
    work = [k for k in range(len(groups)) if centre[k] == rank]
    first = groups[mine][0] == rank

    dests = [centre[mine]] + (list(asm) if work else []) + (serve[rank] if rank in asm else [])
    allowed = topo.mask(core, cores[dests[0]])
    for d in dests:
        allowed &= topo.mask(core, cores[d])
    n = min(NENG, bin(allowed).count("1"))
    eng = _engines(allowed, n)
    h = n // 2
    halves = (_engines(eng, h), eng & ~_engines(eng, h))

    def dst(r):
        rid, pid = topo.addr(cores[r], core)
        return DstId(rid=rid, pnc=pid)

    def one_chip(a, b):
        return topo.host(a) == topo.host(b) and topo.chip(a) == topo.chip(b)

    g.sync.dma_start(out=T.xd[:, :], in_=T.x[:, :]).then_inc(S.ld, 16)
    if first:
        g.scalar.dma_start(out=T.wd[:, :], in_=T.w[:, :]).then_inc(S.ldw, 16)
    rid, pid = topo.addr(cores[centre[mine]], core)
    slot = groups[mine].index(rank)
    g.wait_ge(S.ld, 16)
    g.remote_dma(out_ap=(T.inX, T.inA, T.inB)[slot][:, :], in_ap=T.xd[:, :],
                 remote_sem=(S.sX, S.sA, S.sB)[slot], local_sem=S.sent,
                 pid=pid, routing_id=rid, dma_engine_mask=eng)
    sent = n
    if first:
        g.wait_ge(S.ldw, 16)
        g.remote_dma(out_ap=T.inW[:, :], in_ap=T.wd[:, :], remote_sem=S.sW, local_sem=S.sent,
                     pid=pid, routing_id=rid, dma_engine_mask=eng)
        sent += n

    v = g.vector
    if work:
        k = work[0]
        v.memset(T.zero[:, :], 0.0).then_inc(S.zs, 1)
        v.wait_ge(S.sA, n)
        v.wait_ge(S.sB, n)
        v.tensor_tensor(out=T.ps1[:, 0:F], in0=T.inA[:, :], in1=T.inB[:, :], op=AluOpType.add).then_inc(S.va, 1)
        v.wait_ge(S.sX, n)
        v.wait_ge(S.va, 1)
        v.tensor_tensor(out=T.ps2[:, 0:F], in0=T.ps1[:, 0:F], in1=T.inX[:, :], op=AluOpType.add).then_inc(S.vb, 1)
        v.wait_ge(S.zs, 1)
        v.wait_ge(S.vb, 1)
        v.tensor_tensor(out=T.tsb[:, :], in0=T.ps2[:, 0:F], in1=T.zero[:, :], op=AluOpType.max).then_inc(S.vt, 1)
        g.tensor.wait_ge(S.sW, n)
        g.tensor.wait_ge(S.vt, 1)
        g.tensor.matmul(out=T.ps3[:, 0:F], lhsT=T.inW[:, :], rhs=T.tsb[:, :], start=True, stop=True).then_inc(S.mm, 1)
        v.wait_ge(S.mm, 1)
        v.tensor_copy(out=T.psb[:, :], in_=T.ps3[:, 0:F]).then_inc(S.cp, 1)
        g.wait_ge(S.cp, 1)
        for sem, land in ((S["parr%d" % k], T.pland[k]), (S["qarr%d" % k], T.pown[:, k * F:(k + 1) * F])):
            g.remote_dma_fused([RemoteDMATransfer(dst_ids=[dst(m)], dma_engine_mask=halves[i], remote_sem=sem,
                                                  srcs=[T.psb[:, :]], dsts=[land], alu_op=0)
                                for i, m in enumerate(asm)], local_sem=S.sent)
            sent += 2 * h

    if rank in asm:
        G = len(groups)
        for k in range(G):
            g.wait_ge(S["parr%d" % k], h)
        near_rs = [r for r in serve[rank] if one_chip(core, cores[r])]
        plane = [r for r in serve[rank] if topo.same_plane(core, cores[r])]
        cable = [r for r in serve[rank] if r not in near_rs and r not in plane]
        spare = ~eng
        for r in near_rs:
            spare &= topo.mask(core, cores[r])

        def fold(rs, e):
            return RemoteDMATransfer(dst_ids=[dst(r) for r in rs], dma_engine_mask=e, remote_sem=S.yarr,
                                     srcs=[T.pland[k] for k in range(G)], dsts=[T.yland[:, :] for r in rs], alu_op=1)

        g.remote_dma_fused([fold(plane, halves[0]), fold(cable, halves[1])], local_sem=S.sent)
        g.remote_dma_fused([fold(near_rs, _engines(spare, n))], local_sem=S.sent)
        sent += 2 * h + n
        v.wait_ge(S.qarr0, h)
        v.wait_ge(S.qarr1, h)
        v.tensor_tensor(out=T.ps1[:, 0:F], in0=T.pown[:, 0:F], in1=T.pown[:, F:2 * F], op=AluOpType.add).then_inc(S.va, 1)
        v.wait_ge(S.qarr2, h)
        v.wait_ge(S.va, 1)
        v.tensor_tensor(out=T.ps2[:, 0:F], in0=T.ps1[:, 0:F], in1=T.pown[:, 2 * F:3 * F], op=AluOpType.add).then_inc(S.vb, 1)
        v.wait_ge(S.qarr3, h)
        v.wait_ge(S.vb, 1)
        v.tensor_tensor(out=T.ysb[:, :], in0=T.ps2[:, 0:F], in1=T.pown[:, 3 * F:4 * F], op=AluOpType.add).then_inc(S.vt, 1)
        g.sync.wait_ge(S.vt, 1)
        g.sync.dma_start(out=T.y[:, :], in_=T.ysb[:, :]).then_inc(S.st, 16)
    else:
        giver = [m for m in asm if rank in serve[m]][0]
        g.sync.wait_ge(S.yarr, n if one_chip(core, cores[giver]) else h)
        g.sync.dma_start(out=T.y[:, :], in_=T.yland[:, :]).then_inc(S.st, 16)
    g.sync.wait_ge(S.st, 16)
    g.wait_ge(S.sent, sent)
